import numpy as np
import ml_dtypes


def mxq(x, axis, fmt="e4m3"):
    dtype, down = {"e4m3": (ml_dtypes.float8_e4m3fn, 7), "e5m2": (ml_dtypes.float8_e5m2, 14)}[fmt]
    v = np.moveaxis(np.asarray(x, np.float32).astype(ml_dtypes.bfloat16).astype(np.float64), axis, -1)
    blocks = v.reshape(v.shape[:-1] + (-1, 32))
    amax = np.abs(blocks).max(-1, keepdims=True)
    byte = np.maximum(np.where(amax > 0, np.frexp(amax)[1] - 1 + 127, 0) - down, 1)
    scale = np.exp2(byte - 127.0)
    codes = (blocks / scale).astype(np.float32).astype(dtype).astype(np.float64)
    return np.moveaxis((codes * scale).reshape(v.shape), -1, axis)


WIDE = False


def mx_kscale(k):
    if not WIDE:
        return np.ones(k)
    levels = np.array([10, -10, 5, -5, 0])
    if k % 512:
        return np.exp2(np.random.permutation(np.resize(levels, k // 32))).repeat(32)
    a = np.empty((k // 512, 16))
    for p in range(k // 512):
        a[p, :8] = np.random.permutation(np.resize(levels, 8))
        for g in range(8):
            far = levels[np.abs(levels - a[p, g]) >= 10]
            a[p, g + 8] = far[np.random.randint(len(far))]
    return np.exp2(a.ravel()).repeat(32)


def f64(x):
    return np.asarray(x).astype(np.float64)


def striped(idx):
    return np.tile(idx.reshape(-1, 16).T, (8, 1)).astype(np.uint16)


def unstriped(offs):
    return offs[:16].T.reshape(-1).astype(np.int64)


E2M1 = np.array([0.0, 0.5, 1.0, 1.5, 2.0, 3.0, 4.0, 6.0, -0.0, -0.5, -1.0, -1.5, -2.0, -3.0, -4.0, -6.0])


def pack_weight(w, fmt):
    k, n = w.shape
    w = f64(np.asarray(w, np.float32).astype(ml_dtypes.bfloat16)).reshape(k // 32, 32, n)
    amax = np.abs(w).max(1)
    if fmt == "e4m3":
        byte = np.frexp(amax)[1] - 1 + 127 - 7
    else:
        mant, ex = np.frexp(amax / 6.0)
        byte = np.where(mant > 0.5, ex, ex - 1) + 127
    byte = np.clip(np.where(amax > 0, byte, 1), 1, 254)
    scaled = (w * np.exp2(127.0 - byte)[:, None, :]).reshape(k, n).astype(np.float32)
    by_word = np.ascontiguousarray(scaled.reshape(k // 512, 128, 4, n).transpose(0, 1, 3, 2))
    if fmt == "e4m3":
        words = by_word.astype(ml_dtypes.float8_e4m3fn).view(np.uint8)
    else:
        c = by_word.astype(ml_dtypes.float4_e2m1fn).view(np.uint8) & 0xF
        words = (c[..., 0::2] | (c[..., 1::2] << 4)).reshape(k // 512, 128, 2 * n)
    return np.ascontiguousarray(words), np.ascontiguousarray(byte.astype(np.uint8).reshape(k // 512, 16, n))


def unpack_weight(words, scales, fmt):
    g, _, n = scales.shape
    words = np.ascontiguousarray(words).reshape(g, 128, n, -1)
    if fmt == "e4m3":
        vals = words.view(ml_dtypes.float8_e4m3fn).astype(np.float64)
    else:
        nib = np.empty((g, 128, n, 4), np.uint8)
        nib[..., 0::2] = words & 0xF
        nib[..., 1::2] = words >> 4
        vals = E2M1[nib]
    vals = vals * np.repeat(np.exp2(scales.astype(np.float64) - 127.0), 8, axis=1)[..., None]
    return vals.transpose(0, 1, 3, 2).reshape(g * 512, n)


def gelu(v):
    return 0.5 * v * (1.0 + np.tanh(np.sqrt(2.0 / np.pi) * (v + 0.044715 * v**3)))


K, H, T, S, P, N = 512, 1024, 4096, 1024, 512, 384


def setup_inputs():
    n = np.random.standard_normal
    s = mx_kscale(K)[:, None]
    u = mx_kscale(H)[:, None]
    tab_words, tab_scales = pack_weight(n((K, T)) * s, "e4m3")
    w2_words, w2_scales = pack_weight(n((K, H)) / np.sqrt(K) / s, "e2m1")
    w4_words, w4_scales = pack_weight(n((H, N)) / np.sqrt(H) / u, "e2m1")
    return {
        "tab_words": tab_words, "tab_scales": tab_scales,
        "offs": striped(np.random.permutation(T)[:S]),
        "pos1": striped(np.random.permutation(S)[:P]),
        "pos2": striped(np.random.permutation(S)[:P]),
        "w1": (1.8 * n((K, H)) / np.sqrt(K) / s).astype(np.float32),
        "w2_words": w2_words, "w2_scales": w2_scales,
        "w3": (1.5 * n((K, H)) / np.sqrt(K) / s).astype(np.float32),
        "gain": (np.exp(0.3 * n(H)) * u[:, 0]).astype(np.float32),
        "corridor": (n(H) * u[:, 0]).astype(np.float32),
        "garden": n((H, P)).astype(np.float32),
        "w4_words": w4_words, "w4_scales": w4_scales,
        "w5": (n((H, N)) / np.sqrt(H) / u).astype(np.float32),
    }


def reference(tab_words, tab_scales, offs, pos1, pos2, w1, w2_words, w2_scales, w3,
              gain, corridor, garden, w4_words, w4_scales, w5):
    v = unpack_weight(tab_words, tab_scales, "e4m3")[:, unstriped(offs)]
    turn = mxq(f64(w1), 0, "e4m3").T @ v
    sway = unpack_weight(w2_words, w2_scales, "e2m1").T @ v
    drift = mxq(f64(w3), 0, "e4m3").T @ v
    h = np.maximum(np.tanh(turn) + np.abs(sway), drift) * f64(gain)[:, None]
    xa = mxq(h[:, unstriped(pos1)] + f64(corridor)[:, None], 0, "e4m3")
    xb = mxq(h[:, unstriped(pos2)] * f64(garden), 0, "e4m3")
    w4 = unpack_weight(w4_words, w4_scales, "e2m1")
    return w4.T @ xa + mxq(f64(w5), 0, "e4m3").T @ xb

@@ -1,0 +1,244 @@
+from contextlib import ExitStack
+
+import concourse.mybir as mybir
+
+K, H, T, S, PICK, N = 512, 1024, 4096, 1024, 512, 384
+FLOPS = 2 * (3 * K * H * S + 2 * H * N * PICK)
+
+F32 = mybir.dt.float32
+BF16 = mybir.dt.bfloat16
+I32 = mybir.dt.int32
+U32 = mybir.dt.uint32
+U16 = mybir.dt.uint16
+U8 = mybir.dt.uint8
+FP8X4 = mybir.dt.float8_e4m3fn_x4
+FP4X4 = mybir.dt.float4_e2m1fn_x4
+ACT = mybir.ActivationFunctionType
+ALU = mybir.AluOpType
+
+P = 128
+PACK = 4
+PASS = P * PACK
+BANK = 512
+BLOCKS = H // PASS
+
+
+def tile_list_wandering_alert_features_kernel(
+    tc, tab_words, tab_scales, offs, pos1, pos2, w1, w2_words, w2_scales, w3,
+    gain, corridor, garden, w4_words, w4_scales, w5, out,
+):
+    nc = tc.nc
+    with ExitStack() as ctx:
+        keep = ctx.enter_context(tc.tile_pool(name="keep", bufs=1))
+        ring = ctx.enter_context(tc.tile_pool(name="ring", bufs=2))
+        psum = ctx.enter_context(tc.psum_pool(name="psum", bufs=1))
+
+        def load_scale_rows(queue, plane, rows):
+            for q in range(4):
+                queue.dma_start(out=plane[32 * q : 32 * q + 4].bitcast(I32), in_=rows[4 * q : 4 * q + 4].bitcast(I32))
+
+        offs_sb = keep.tile([P, S // 16], U16, name="offs_sb")
+        pos1_sb = keep.tile([P, PICK // 16], U16, name="pos1_sb")
+        pos2_sb = keep.tile([P, PICK // 16], U16, name="pos2_sb")
+        tab_w = keep.tile([P, T], U32, name="tab_w", align_bytes=64)
+        tab_s = keep.tile([P, T], U8, name="tab_s", align_bytes=64)
+        w2_raw = keep.tile([P, 2 * H], U8, name="w2_raw", align_bytes=64)
+        w2_sraw = keep.tile([P, H], U8, name="w2_sraw", align_bytes=64)
+        w4_w = keep.tile([P, BLOCKS, 2 * N], U8, name="w4_w", align_bytes=64)
+        w4_s = keep.tile([P, BLOCKS, N], U8, name="w4_s", align_bytes=64)
+        gain_sb = keep.tile([P, BLOCKS, PACK], F32, name="gain_sb")
+        corr_sb = keep.tile([P, BLOCKS, PACK], F32, name="corr_sb")
+
+        nc.vector.memset(tab_s[:].bitcast(I32), 0)
+        nc.vector.memset(w2_sraw[:].bitcast(I32), 0)
+        nc.vector.memset(w4_s[:].bitcast(I32), 0)
+
+        def load_w(w, b, name):
+            raw = keep.tile([P, PACK, PASS], F32, name=name)
+            nc.sync.dma_start(out=raw[:], in_=w[:, b * PASS : (b + 1) * PASS].rearrange("(p j) c -> p j c", j=PACK))
+            return raw
+
+        def load_rows(x, b, name):
+            raw = keep.tile([P, PACK, x.shape[1]], F32, name=name)
+            nc.sync.dma_start(out=raw[:], in_=x[b * PASS : (b + 1) * PASS, :].rearrange("(p j) c -> p j c", j=PACK))
+            return raw
+
+        nc.sync.dma_start(offs_sb[:], offs)
+        nc.sync.dma_start(out=w2_raw[:].bitcast(I32), in_=w2_words[0].bitcast(I32))
+        w1_raw = [load_w(w1, 0, "w1_raw0")]
+        nc.sync.dma_start(out=tab_w[:].bitcast(I32), in_=tab_words[0].rearrange("p n t -> p (n t)").bitcast(I32))
+        load_scale_rows(nc.gpsimd, tab_s, tab_scales[0])
+        load_scale_rows(nc.gpsimd, w2_sraw, w2_scales[0])
+        w3_raw = [load_w(w3, 0, "w3_raw0")]
+        nc.sync.dma_start(pos1_sb[:], pos1)
+        nc.sync.dma_start(pos2_sb[:], pos2)
+        nc.sync.dma_start(out=gain_sb[:], in_=gain.rearrange("(b p t) -> p b t", b=BLOCKS, t=PACK))
+        nc.sync.dma_start(out=corr_sb[:], in_=corridor.rearrange("(b p t) -> p b t", b=BLOCKS, t=PACK))
+        garden_sb = [load_rows(garden, 0, "garden0")]
+        w1_raw.append(load_w(w1, 1, "w1_raw1"))
+        w3_raw.append(load_w(w3, 1, "w3_raw1"))
+        garden_sb.append(load_rows(garden, 1, "garden1"))
+        w5_raw = [load_rows(w5, b, "w5_raw%d" % b) for b in range(BLOCKS)]
+        nc.sync.dma_start(out=w4_w[:].bitcast(I32), in_=w4_words.rearrange("a p n -> p a n").bitcast(I32))
+        load_scale_rows(nc.sync, w4_s, w4_scales.rearrange("a r n -> r a n"))
+
+        def copy_on(engine, dst, src):
+            if engine is nc.scalar:
+                nc.scalar.copy(out=dst, in_=src)
+            else:
+                engine.tensor_copy(out=dst, in_=src)
+
+        def quantise(grouped, name):
+            width = grouped.shape[1] // PACK
+            codes = keep.tile([P, width], U32, name=name + "_c", align_bytes=64)
+            scales = keep.tile([P, width], U8, name=name + "_s", align_bytes=64)
+            nc.vector.quantize_mx(out=codes[:].bitcast(FP8X4), scales=scales[:], in_=grouped[:])
+            return codes, scales
+
+        def deal_weight(engine, raw):
+            grouped = ring.tile([P, PACK * PASS], BF16, name="w_grouped", align_bytes=64)
+            copy_on(
+                engine,
+                grouped[:].rearrange("p (t m j) -> p m t j", t=PACK, j=PACK),
+                raw[:].rearrange("p j (m t) -> p m t j", t=PACK),
+            )
+            return grouped
+
+        def interleave(engine, planes, name):
+            width = planes.shape[2]
+            grouped = ring.tile([P, PACK * width], BF16, name=name, align_bytes=64)
+            copy_on(
+                engine,
+                grouped[:].rearrange("p (c i t) -> p c t i", i=4, t=PACK),
+                planes[:].rearrange("p t (c i) -> p c t i", i=4),
+            )
+            return grouped
+
+        w2_w = keep.tile([P, 2 * H], U8, name="w2_w", align_bytes=64)
+        w2_s = keep.tile([P, H], U8, name="w2_s", align_bytes=64)
+        nc.vector.tensor_copy(
+            out=w2_w[:].bitcast(U16).rearrange("p (b t m) -> p b m t", b=BLOCKS, t=PACK),
+            in_=w2_raw[:].bitcast(U16).rearrange("p (b m t) -> p b m t", b=BLOCKS, t=PACK),
+        )
+        w1_q = [quantise(deal_weight(nc.scalar, w1_raw[0]), "w1q0")]
+
+        v_s = [keep.tile([P, BANK], U8, name="v_s%d" % h, align_bytes=64) for h in range(2)]
+        v_w = [keep.tile([P, BANK], U32, name="v_w%d" % h, align_bytes=64) for h in range(2)]
+        cols = BANK // 16
+        for h in range(2):
+            nc.vector.tensor_copy(v_s[h][:], tab_s[:].indirect(offs_sb[:, h * cols : (h + 1) * cols]))
+        nc.vector.tensor_copy(
+            out=w2_s[:].rearrange("p (b t m) -> p b m t", b=BLOCKS, t=PACK),
+            in_=w2_sraw[:].rearrange("p (b m t) -> p b m t", b=BLOCKS, t=PACK),
+        )
+        for h in range(2):
+            nc.vector.tensor_copy(v_w[h][:], tab_w[:].indirect(offs_sb[:, h * cols : (h + 1) * cols]))
+        w3_q = [quantise(deal_weight(nc.vector, w3_raw[0]), "w3q0")]
+
+        def product(tag, bufs, lhs, lhs_scale, h):
+            bank = psum.tile([P, BANK], F32, name=tag, tag=tag, bufs=bufs)
+            nc.tensor.matmul_mx(
+                out=bank[:], lhsT=lhs, lhsT_scale=lhs_scale,
+                rhs=v_w[h][:].bitcast(FP8X4), rhs_scale=v_s[h][:], start=True, stop=True,
+            )
+            return bank
+
+        def unary(i):
+            b, t = divmod(i, PACK)
+            m = slice(t * P, (t + 1) * P)
+            c0 = i * P
+            th = ring.tile([P, S], F32, name="th")
+            ab = ring.tile([P, S], F32, name="ab")
+            for h in range(2):
+                hs = slice(h * BANK, (h + 1) * BANK)
+                turn = product("turn", 3, w1_q[b][0][:, m].bitcast(FP8X4), w1_q[b][1][:, m], h)
+                sway = product("sway", 2, w2_w[:, 2 * c0 : 2 * (c0 + P)].bitcast(FP4X4), w2_s[:, c0 : c0 + P], h)
+                nc.scalar.activation(out=th[:, hs], in_=turn[:], func=ACT.Tanh)
+                nc.scalar.activation(out=ab[:, hs], in_=sway[:], func=ACT.Abs)
+            return th, ab
+
+        def add(th, ab):
+            u = ring.tile([P, S], F32, name="u")
+            nc.vector.tensor_tensor(out=u[:], in0=th[:], in1=ab[:], op=ALU.add)
+            return u
+
+        def maximum(i, u):
+            b, t = divmod(i, PACK)
+            m = slice(t * P, (t + 1) * P)
+            top = ring.tile([P, S], F32, name="top", bufs=3)
+            for h in range(2):
+                hs = slice(h * BANK, (h + 1) * BANK)
+                drift = product("drift", 3, w3_q[b][0][:, m].bitcast(FP8X4), w3_q[b][1][:, m], h)
+                nc.vector.tensor_tensor(out=top[:, hs], in0=drift[:], in1=u[:, hs], op=ALU.max)
+            return top
+
+        xa_planes = [keep.tile([P, PACK, PICK], BF16, name="xa_planes%d" % b) for b in range(BLOCKS)]
+        xb_planes = [keep.tile([P, PACK, PICK], F32, name="xb_planes%d" % b) for b in range(BLOCKS)]
+
+        def scale_garden(i):
+            b, t = divmod(i, PACK)
+            gg = ring.tile([P, PICK], F32, name="gg", bufs=3)
+            nc.scalar.activation(out=gg[:], in_=garden_sb[b][:, t, :], func=ACT.Copy, scale=gain_sb[:, b, t : t + 1])
+            return gg
+
+        def pick_a(i, top):
+            b, t = divmod(i, PACK)
+            ga = ring.tile([P, PICK], F32, name="ga")
+            nc.vector.tensor_copy(ga[:], top[:].indirect(pos1_sb[:]))
+            nc.scalar.activation(
+                out=xa_planes[b][:, t, :], in_=ga[:], func=ACT.Identity,
+                scale=gain_sb[:, b, t : t + 1], bias=corr_sb[:, b, t : t + 1],
+            )
+
+        def pick_b(i, top, gg):
+            b, t = divmod(i, PACK)
+            nc.vector.tensor_tensor(xb_planes[b][:, t, :], top[:].indirect(pos2_sb[:]), gg[:], ALU.mult)
+
+        xa_q, xb_q, w5_q = [], [], []
+        tiles = BLOCKS * PACK
+        un = {0: unary(0)}
+        tops = {}
+        ggs = {}
+        for i in range(tiles + 1):
+            if i < tiles:
+                u = add(*un[i])
+                ggs[i] = scale_garden(i)
+            if i + 1 < tiles:
+                un[i + 1] = unary(i + 1)
+            if i >= 1:
+                pick_a(i - 1, tops[i - 1])
+            if i < tiles:
+                tops[i] = maximum(i, u)
+            if i >= 1:
+                pick_b(i - 1, tops[i - 1], ggs[i - 1])
+            if i == 1:
+                w1_q.append(quantise(deal_weight(nc.scalar, w1_raw[1]), "w1q1"))
+            if i == 2:
+                w3_q.append(quantise(deal_weight(nc.scalar, w3_raw[1]), "w3q1"))
+            if i in (5, 6):
+                w5_q.append(quantise(interleave(nc.scalar, w5_raw[i - 5], "w5_grouped"), "w5q%d" % (i - 5)))
+            if i % PACK == 0 and i > 0:
+                b = i // PACK - 1
+                ga4 = interleave(nc.scalar, xa_planes[b], "xa_grouped")
+                gb4 = interleave(nc.vector, xb_planes[b], "xb_grouped")
+                xb_q.append(quantise(gb4, "xbq%d" % b))
+                xa_q.append(quantise(ga4, "xaq%d" % b))
+
+        outs = [psum.tile([P, PICK], F32, name="out_bank%d" % n, tag="turn", bufs=3) for n in range(N // P)]
+        for b in range(BLOCKS):
+            for n in range(N // P):
+                m = slice(n * P, (n + 1) * P)
+                nc.tensor.matmul_mx(
+                    out=outs[n][:], lhsT=w5_q[b][0][:, m].bitcast(FP8X4), lhsT_scale=w5_q[b][1][:, m],
+                    rhs=xb_q[b][0][:].bitcast(FP8X4), rhs_scale=xb_q[b][1][:], start=(b == 0), stop=False,
+                )
+            for n in range(N // P):
+                nc.tensor.matmul_mx(
+                    out=outs[n][:], lhsT=w4_w[:, b, 2 * n * P : 2 * (n + 1) * P].bitcast(FP4X4),
+                    lhsT_scale=w4_s[:, b, n * P : (n + 1) * P],
+                    rhs=xa_q[b][0][:].bitcast(FP8X4), rhs_scale=xa_q[b][1][:], start=False, stop=(b == BLOCKS - 1),
+                )
+        for n in range(N // P):
+            res = ring.tile([P, PICK], F32, name="res", bufs=3)
+            copy_on(nc.vector if n == 1 else nc.scalar, res[:], outs[n][:])
+            nc.sync.dma_start(out=out[n * P : (n + 1) * P, :], in_=res[:])

@@ -65,10 +65,10 @@ def tile_list_wandering_alert_features_kernel(
 
         nc.sync.dma_start(offs_sb[:], offs)
         nc.sync.dma_start(out=w2_raw[:].bitcast(I32), in_=w2_words[0].bitcast(I32))
+        load_scale_rows(nc.sync, tab_s, tab_scales[0])
         w1_raw = [load_w(w1, 0, "w1_raw0")]
         nc.sync.dma_start(out=tab_w[:].bitcast(I32), in_=tab_words[0].rearrange("p n t -> p (n t)").bitcast(I32))
-        load_scale_rows(nc.gpsimd, tab_s, tab_scales[0])
-        load_scale_rows(nc.gpsimd, w2_sraw, w2_scales[0])
+        load_scale_rows(nc.scalar, w2_sraw, w2_scales[0])
         w3_raw = [load_w(w3, 0, "w3_raw0")]
         nc.sync.dma_start(pos1_sb[:], pos1)
         nc.sync.dma_start(pos2_sb[:], pos2)
@@ -106,11 +106,11 @@ def tile_list_wandering_alert_features_kernel(
 
         def interleave(engine, planes, name):
             width = planes.shape[2]
-            grouped = ring.tile([P, PACK * width], BF16, name=name, align_bytes=64)
+            grouped = ring.tile([P, PACK * width], BF16, name=name, align_bytes=64, bufs=3)
             copy_on(
                 engine,
                 grouped[:].rearrange("p (c i t) -> p c t i", i=4, t=PACK),
-                planes[:].rearrange("p t (c i) -> p c t i", i=4),
+                planes.rearrange("p t (c i) -> p c t i", i=4),
             )
             return grouped
 
@@ -120,7 +120,7 @@ def tile_list_wandering_alert_features_kernel(
             out=w2_w[:].bitcast(U16).rearrange("p (b t m) -> p b m t", b=BLOCKS, t=PACK),
             in_=w2_raw[:].bitcast(U16).rearrange("p (b m t) -> p b m t", b=BLOCKS, t=PACK),
         )
-        w1_q = [quantise(deal_weight(nc.scalar, w1_raw[0]), "w1q0")]
+        w1_grouped = deal_weight(nc.scalar, w1_raw[0])
 
         v_s = [keep.tile([P, BANK], U8, name="v_s%d" % h, align_bytes=64) for h in range(2)]
         v_w = [keep.tile([P, BANK], U32, name="v_w%d" % h, align_bytes=64) for h in range(2)]
@@ -131,6 +131,7 @@ def tile_list_wandering_alert_features_kernel(
             out=w2_s[:].rearrange("p (b t m) -> p b m t", b=BLOCKS, t=PACK),
             in_=w2_sraw[:].rearrange("p (b m t) -> p b m t", b=BLOCKS, t=PACK),
         )
+        w1_q = [quantise(w1_grouped, "w1q0")]
         for h in range(2):
             nc.vector.tensor_copy(v_w[h][:], tab_w[:].indirect(offs_sb[:, h * cols : (h + 1) * cols]))
         w3_q = [quantise(deal_weight(nc.vector, w3_raw[0]), "w3q0")]
@@ -158,19 +159,19 @@ def tile_list_wandering_alert_features_kernel(
             return th, ab
 
         def add(th, ab):
-            u = ring.tile([P, S], F32, name="u")
-            nc.vector.tensor_tensor(out=u[:], in0=th[:], in1=ab[:], op=ALU.add)
-            return u
-
-        def maximum(i, u):
-            b, t = divmod(i, PACK)
-            m = slice(t * P, (t + 1) * P)
             top = ring.tile([P, S], F32, name="top", bufs=3)
             for h in range(2):
                 hs = slice(h * BANK, (h + 1) * BANK)
-                drift = product("drift", 3, w3_q[b][0][:, m].bitcast(FP8X4), w3_q[b][1][:, m], h)
-                nc.vector.tensor_tensor(out=top[:, hs], in0=drift[:], in1=u[:, hs], op=ALU.max)
+                nc.gpsimd.tensor_tensor(out=top[:, hs], in0=th[:, hs], in1=ab[:, hs], op=ALU.add)
             return top
+
+        def maximum(i, top):
+            b, t = divmod(i, PACK)
+            m = slice(t * P, (t + 1) * P)
+            for h in range(2):
+                hs = slice(h * BANK, (h + 1) * BANK)
+                drift = product("drift", 3, w3_q[b][0][:, m].bitcast(FP8X4), w3_q[b][1][:, m], h)
+                nc.vector.tensor_tensor(out=top[:, hs], in0=drift[:], in1=top[:, hs], op=ALU.max)
 
         xa_planes = [keep.tile([P, PACK, PICK], BF16, name="xa_planes%d" % b) for b in range(BLOCKS)]
         xb_planes = [keep.tile([P, PACK, PICK], F32, name="xb_planes%d" % b) for b in range(BLOCKS)]
@@ -181,64 +182,87 @@ def tile_list_wandering_alert_features_kernel(
             nc.scalar.activation(out=gg[:], in_=garden_sb[b][:, t, :], func=ACT.Copy, scale=gain_sb[:, b, t : t + 1])
             return gg
 
-        def pick_a(i, top):
+        def pick_a(i, top, c0, c1):
             b, t = divmod(i, PACK)
-            ga = ring.tile([P, PICK], F32, name="ga")
-            nc.vector.tensor_copy(ga[:], top[:].indirect(pos1_sb[:]))
+            ga = ring.tile([P, c1 - c0], F32, name="ga")
+            nc.vector.tensor_copy(ga[:], top[:].indirect(pos1_sb[:, c0 // 16 : c1 // 16]))
             nc.scalar.activation(
-                out=xa_planes[b][:, t, :], in_=ga[:], func=ACT.Identity,
+                out=xa_planes[b][:, t, c0:c1], in_=ga[:], func=ACT.Identity,
                 scale=gain_sb[:, b, t : t + 1], bias=corr_sb[:, b, t : t + 1],
             )
 
-        def pick_b(i, top, gg):
+        def pick_b(i, top, gg, c0, c1):
             b, t = divmod(i, PACK)
-            nc.vector.tensor_tensor(xb_planes[b][:, t, :], top[:].indirect(pos2_sb[:]), gg[:], ALU.mult)
+            nc.vector.tensor_tensor(
+                xb_planes[b][:, t, c0:c1], top[:].indirect(pos2_sb[:, c0 // 16 : c1 // 16]), gg[:, c0:c1], ALU.mult
+            )
 
-        xa_q, xb_q, w5_q = [], [], []
+        w5_q = []
         tiles = BLOCKS * PACK
-        un = {0: unary(0)}
-        tops = {}
+        tops = {0: add(*unary(0))}
         ggs = {}
-        for i in range(tiles + 1):
-            if i < tiles:
-                u = add(*un[i])
-                ggs[i] = scale_garden(i)
+        for i in range(tiles):
+            ggs[i] = scale_garden(i)
             if i + 1 < tiles:
-                un[i + 1] = unary(i + 1)
+                tops[i + 1] = add(*unary(i + 1))
+            maximum(i, tops[i])
             if i >= 1:
-                pick_a(i - 1, tops[i - 1])
-            if i < tiles:
-                tops[i] = maximum(i, u)
-            if i >= 1:
-                pick_b(i - 1, tops[i - 1], ggs[i - 1])
+                pick_a(i - 1, tops[i - 1], 0, PICK)
             if i == 1:
                 w1_q.append(quantise(deal_weight(nc.scalar, w1_raw[1]), "w1q1"))
             if i == 2:
-                w3_q.append(quantise(deal_weight(nc.scalar, w3_raw[1]), "w3q1"))
-            if i in (5, 6):
-                w5_q.append(quantise(interleave(nc.scalar, w5_raw[i - 5], "w5_grouped"), "w5q%d" % (i - 5)))
-            if i % PACK == 0 and i > 0:
-                b = i // PACK - 1
-                ga4 = interleave(nc.scalar, xa_planes[b], "xa_grouped")
-                gb4 = interleave(nc.vector, xb_planes[b], "xb_grouped")
-                xb_q.append(quantise(gb4, "xbq%d" % b))
-                xa_q.append(quantise(ga4, "xaq%d" % b))
+                w3_q.append(quantise(deal_weight(nc.vector, w3_raw[1]), "w3q1"))
+            if i == 5:
+                xa0 = quantise(interleave(nc.scalar, xa_planes[0][:], "xa_grouped"), "xaq0")
+            if i == 6:
+                xb0 = quantise(interleave(nc.vector, xb_planes[0][:], "xb_grouped"), "xbq0")
+            if i in (3, 7):
+                w5_q.append(quantise(interleave(nc.scalar, w5_raw[i // 7][:], "w5_grouped"), "w5q%d" % (i // 7)))
+            if i >= 1:
+                pick_b(i - 1, tops[i - 1], ggs[i - 1], 0, PICK)
 
-        outs = [psum.tile([P, PICK], F32, name="out_bank%d" % n, tag="turn", bufs=3) for n in range(N // P)]
-        for b in range(BLOCKS):
+        half = PICK // 2
+        last = tiles - 1
+        tags = [("turn", 3)] * 3 + [("sway", 2)] * 2 + [("drift", 3)]
+        outs = [psum.tile([P, half], F32, name="out_bank%d" % k, tag=tag, bufs=bufs) for k, (tag, bufs) in enumerate(tags)]
+
+        def passes_b(h, b, codes, scales, start):
             for n in range(N // P):
                 m = slice(n * P, (n + 1) * P)
                 nc.tensor.matmul_mx(
-                    out=outs[n][:], lhsT=w5_q[b][0][:, m].bitcast(FP8X4), lhsT_scale=w5_q[b][1][:, m],
-                    rhs=xb_q[b][0][:].bitcast(FP8X4), rhs_scale=xb_q[b][1][:], start=(b == 0), stop=False,
+                    out=outs[3 * h + n][:], lhsT=w5_q[b][0][:, m].bitcast(FP8X4), lhsT_scale=w5_q[b][1][:, m],
+                    rhs=codes.bitcast(FP8X4), rhs_scale=scales, start=start, stop=False,
                 )
+
+        def passes_a(h, b, codes, scales, stop):
             for n in range(N // P):
                 nc.tensor.matmul_mx(
-                    out=outs[n][:], lhsT=w4_w[:, b, 2 * n * P : 2 * (n + 1) * P].bitcast(FP4X4),
+                    out=outs[3 * h + n][:], lhsT=w4_w[:, b, 2 * n * P : 2 * (n + 1) * P].bitcast(FP4X4),
                     lhsT_scale=w4_s[:, b, n * P : (n + 1) * P],
-                    rhs=xa_q[b][0][:].bitcast(FP8X4), rhs_scale=xa_q[b][1][:], start=False, stop=(b == BLOCKS - 1),
+                    rhs=codes.bitcast(FP8X4), rhs_scale=scales, start=False, stop=stop,
                 )
-        for n in range(N // P):
-            res = ring.tile([P, PICK], F32, name="res", bufs=3)
-            copy_on(nc.vector if n == 1 else nc.scalar, res[:], outs[n][:])
-            nc.sync.dma_start(out=out[n * P : (n + 1) * P, :], in_=res[:])
+
+        for h in range(2):
+            hs = slice(h * half, (h + 1) * half)
+            passes_b(h, 0, xb0[0][:, hs], xb0[1][:, hs], True)
+            passes_a(h, 0, xa0[0][:, hs], xa0[1][:, hs], False)
+        for h in range(2):
+            pick_a(last, tops[last], h * half, (h + 1) * half)
+            pick_b(last, tops[last], ggs[last], h * half, (h + 1) * half)
+        grouped = []
+        for h in range(2):
+            hs = slice(h * half, (h + 1) * half)
+            grouped.append((
+                interleave(nc.scalar, xa_planes[1][:, :, hs], "xa_grouped"),
+                interleave(nc.vector, xb_planes[1][:, :, hs], "xb_grouped"),
+            ))
+        for h in range(2):
+            hs = slice(h * half, (h + 1) * half)
+            xb1 = quantise(grouped[h][1], "xbq1%d" % h)
+            xa1 = quantise(grouped[h][0], "xaq1%d" % h)
+            passes_b(h, 1, xb1[0][:], xb1[1][:], False)
+            passes_a(h, 1, xa1[0][:], xa1[1][:], True)
+            for n in range(N // P):
+                res = ring.tile([P, half], F32, name="res", bufs=6)
+                copy_on(nc.vector if (h == 1 and n == 1) else nc.scalar, res[:], outs[3 * h + n][:])
+                nc.sync.dma_start(out=out[n * P : (n + 1) * P, hs], in_=res[:])

@@ -1,6 +1,7 @@
 from contextlib import ExitStack
 
 import concourse.mybir as mybir
+from concourse.masks import make_identity
 
 K, H, T, S, PICK, N = 512, 1024, 4096, 1024, 512, 384
 FLOPS = 2 * (3 * K * H * S + 2 * H * N * PICK)
@@ -65,10 +66,10 @@ def tile_list_wandering_alert_features_kernel(
 
         nc.sync.dma_start(offs_sb[:], offs)
         nc.sync.dma_start(out=w2_raw[:].bitcast(I32), in_=w2_words[0].bitcast(I32))
-        load_scale_rows(nc.sync, tab_s, tab_scales[0])
         w1_raw = [load_w(w1, 0, "w1_raw0")]
+        load_scale_rows(nc.sync, tab_s, tab_scales[0])
         nc.sync.dma_start(out=tab_w[:].bitcast(I32), in_=tab_words[0].rearrange("p n t -> p (n t)").bitcast(I32))
-        load_scale_rows(nc.scalar, w2_sraw, w2_scales[0])
+        load_scale_rows(nc.sync, w2_sraw, w2_scales[0])
         w3_raw = [load_w(w3, 0, "w3_raw0")]
         nc.sync.dma_start(pos1_sb[:], pos1)
         nc.sync.dma_start(pos2_sb[:], pos2)
@@ -106,7 +107,7 @@ def tile_list_wandering_alert_features_kernel(
 
         def interleave(engine, planes, name):
             width = planes.shape[2]
-            grouped = ring.tile([P, PACK * width], BF16, name=name, align_bytes=64, bufs=3)
+            grouped = ring.tile([P, PACK * width], BF16, name=name, align_bytes=64)
             copy_on(
                 engine,
                 grouped[:].rearrange("p (c i t) -> p c t i", i=4, t=PACK),
@@ -127,58 +128,66 @@ def tile_list_wandering_alert_features_kernel(
         cols = BANK // 16
         for h in range(2):
             nc.vector.tensor_copy(v_s[h][:], tab_s[:].indirect(offs_sb[:, h * cols : (h + 1) * cols]))
-        nc.vector.tensor_copy(
-            out=w2_s[:].rearrange("p (b t m) -> p b m t", b=BLOCKS, t=PACK),
-            in_=w2_sraw[:].rearrange("p (b m t) -> p b m t", b=BLOCKS, t=PACK),
-        )
         w1_q = [quantise(w1_grouped, "w1q0")]
-        for h in range(2):
-            nc.vector.tensor_copy(v_w[h][:], tab_w[:].indirect(offs_sb[:, h * cols : (h + 1) * cols]))
+
+        def deal_w2_scales(b):
+            cs = slice(b * PASS, (b + 1) * PASS)
+            nc.vector.tensor_copy(
+                out=w2_s[:, cs].rearrange("p (t m) -> p m t", t=PACK),
+                in_=w2_sraw[:, cs].rearrange("p (m t) -> p m t", t=PACK),
+            )
+
+        nc.vector.tensor_copy(v_w[0][:], tab_w[:].indirect(offs_sb[:, 0:cols]))
+        deal_w2_scales(0)
+        nc.vector.tensor_copy(v_w[1][:], tab_w[:].indirect(offs_sb[:, cols : 2 * cols]))
         w3_q = [quantise(deal_weight(nc.vector, w3_raw[0]), "w3q0")]
 
-        def product(tag, bufs, lhs, lhs_scale, h):
-            bank = psum.tile([P, BANK], F32, name=tag, tag=tag, bufs=bufs)
+        ident = keep.tile([P, P], F32, name="ident")
+        make_identity(nc, ident[:])
+
+        def first_stage(i, h, top):
+            b, t = divmod(i, PACK)
+            m = slice(t * P, (t + 1) * P)
+            hs = slice(h * BANK, (h + 1) * BANK)
+            turn = psum.tile([P, BANK], F32, name="turn", tag="turn", bufs=2)
+            sway = psum.tile([P, BANK], F32, name="sway", tag="sway", bufs=2)
+            drift = psum.tile([P, BANK], F32, name="drift", tag="drift", bufs=2)
+            for bank, words, scales in (
+                (turn, w1_q[b][0][:, m].bitcast(FP8X4), w1_q[b][1][:, m]),
+                (sway, w2_w[:, 2 * i * P : 2 * (i + 1) * P].bitcast(FP4X4), w2_s[:, i * P : (i + 1) * P]),
+            ):
+                for q in range(BANK // P):
+                    js = slice(q * P, (q + 1) * P)
+                    nc.tensor.matmul_mx(
+                        out=bank[:, js], lhsT=v_w[h][:, js].bitcast(FP8X4), lhsT_scale=v_s[h][:, js],
+                        rhs=words, rhs_scale=scales, start=True, stop=True,
+                    )
             nc.tensor.matmul_mx(
-                out=bank[:], lhsT=lhs, lhsT_scale=lhs_scale,
+                out=drift[:], lhsT=w3_q[b][0][:, m].bitcast(FP8X4), lhsT_scale=w3_q[b][1][:, m],
                 rhs=v_w[h][:].bitcast(FP8X4), rhs_scale=v_s[h][:], start=True, stop=True,
             )
-            return bank
-
-        def unary(i):
-            b, t = divmod(i, PACK)
-            m = slice(t * P, (t + 1) * P)
-            c0 = i * P
-            th = ring.tile([P, S], F32, name="th")
-            ab = ring.tile([P, S], F32, name="ab")
-            for h in range(2):
-                hs = slice(h * BANK, (h + 1) * BANK)
-                turn = product("turn", 3, w1_q[b][0][:, m].bitcast(FP8X4), w1_q[b][1][:, m], h)
-                sway = product("sway", 2, w2_w[:, 2 * c0 : 2 * (c0 + P)].bitcast(FP4X4), w2_s[:, c0 : c0 + P], h)
-                nc.scalar.activation(out=th[:, hs], in_=turn[:], func=ACT.Tanh)
-                nc.scalar.activation(out=ab[:, hs], in_=sway[:], func=ACT.Abs)
+            th = ring.tile([P, BANK], F32, name="th", bufs=3)
+            ab = ring.tile([P, BANK], F32, name="ab", bufs=3)
+            nc.scalar.activation(out=th[:], in_=turn[:], func=ACT.Tanh)
+            nc.scalar.activation(out=ab[:], in_=sway[:], func=ACT.Abs)
+            nc.scalar.copy(out=top[:, hs], in_=drift[:])
             return th, ab
 
-        def add(th, ab):
-            top = ring.tile([P, S], F32, name="top", bufs=3)
-            for h in range(2):
-                hs = slice(h * BANK, (h + 1) * BANK)
-                nc.gpsimd.tensor_tensor(out=top[:, hs], in0=th[:, hs], in1=ab[:, hs], op=ALU.add)
-            return top
-
-        def maximum(i, top):
-            b, t = divmod(i, PACK)
-            m = slice(t * P, (t + 1) * P)
-            for h in range(2):
-                hs = slice(h * BANK, (h + 1) * BANK)
-                drift = product("drift", 3, w3_q[b][0][:, m].bitcast(FP8X4), w3_q[b][1][:, m], h)
-                nc.vector.tensor_tensor(out=top[:, hs], in0=drift[:], in1=top[:, hs], op=ALU.max)
+        def maximum(h, top, th, ab):
+            hs = slice(h * BANK, (h + 1) * BANK)
+            total = psum.tile([P, BANK], F32, name="total", bufs=2)
+            for q in range(BANK // P):
+                js = slice(q * P, (q + 1) * P)
+                nc.tensor.matmul(total[:, js], lhsT=th[:, js], rhs=ident[:], is_transpose=True, start=True, stop=False)
+                nc.tensor.matmul(total[:, js], lhsT=ab[:, js], rhs=ident[:], is_transpose=True, start=False, stop=True)
+            nc.vector.tensor_tensor(out=top[:, hs], in0=total[:], in1=top[:, hs], op=ALU.max)
 
         xa_planes = [keep.tile([P, PACK, PICK], BF16, name="xa_planes%d" % b) for b in range(BLOCKS)]
         xb_planes = [keep.tile([P, PACK, PICK], F32, name="xb_planes%d" % b) for b in range(BLOCKS)]
 
         def scale_garden(i):
             b, t = divmod(i, PACK)
-            gg = ring.tile([P, PICK], F32, name="gg", bufs=3)
+            gg = ring.tile([P, PICK], F32, name="gg", bufs=4)
             nc.scalar.activation(out=gg[:], in_=garden_sb[b][:, t, :], func=ACT.Copy, scale=gain_sb[:, b, t : t + 1])
             return gg
 
@@ -199,31 +208,41 @@ def tile_list_wandering_alert_features_kernel(
 
         w5_q = []
         tiles = BLOCKS * PACK
-        tops = {0: add(*unary(0))}
+        tops = {}
         ggs = {}
-        for i in range(tiles):
-            ggs[i] = scale_garden(i)
-            if i + 1 < tiles:
-                tops[i + 1] = add(*unary(i + 1))
-            maximum(i, tops[i])
-            if i >= 1:
+        parts = {}
+        for k in range(2 * tiles + 1):
+            i, h = divmod(k, 2)
+            if i < tiles:
+                if h == 0:
+                    tops[i] = ring.tile([P, S], F32, name="top", bufs=3)
+                parts[k] = first_stage(i, h, tops[i])
+            if k >= 1:
+                maximum((k - 1) % 2, tops[(k - 1) // 2], *parts[k - 1])
+            if h == 0 and i < tiles:
+                ggs[i] = scale_garden(i)
+            if h == 1 and i >= 1:
                 pick_a(i - 1, tops[i - 1], 0, PICK)
-            if i == 1:
-                w1_q.append(quantise(deal_weight(nc.scalar, w1_raw[1]), "w1q1"))
-            if i == 2:
+            if k == 1:
+                deal_w2_scales(1)
+            if k == 3:
+                w1_q.append(quantise(deal_weight(nc.vector, w1_raw[1]), "w1q1"))
+            if k == 5:
                 w3_q.append(quantise(deal_weight(nc.vector, w3_raw[1]), "w3q1"))
-            if i == 5:
-                xa0 = quantise(interleave(nc.scalar, xa_planes[0][:], "xa_grouped"), "xaq0")
-            if i == 6:
+            if k == 11:
+                xa0 = quantise(interleave(nc.vector, xa_planes[0][:], "xa_grouped"), "xaq0")
+            if k == 13:
                 xb0 = quantise(interleave(nc.vector, xb_planes[0][:], "xb_grouped"), "xbq0")
-            if i in (3, 7):
-                w5_q.append(quantise(interleave(nc.scalar, w5_raw[i // 7][:], "w5_grouped"), "w5q%d" % (i // 7)))
-            if i >= 1:
-                pick_b(i - 1, tops[i - 1], ggs[i - 1], 0, PICK)
+            if k == 7:
+                w5_q.append(quantise(interleave(nc.scalar, w5_raw[0][:], "w5_grouped0"), "w5q0"))
+            if k == 9:
+                w5_q.append(quantise(interleave(nc.scalar, w5_raw[1][:], "w5_grouped1"), "w5q1"))
+            if h == 0 and 2 <= i:
+                pick_b(i - 2, tops[i - 2], ggs[i - 2], 0, PICK)
 
         half = PICK // 2
         last = tiles - 1
-        tags = [("turn", 3)] * 3 + [("sway", 2)] * 2 + [("drift", 3)]
+        tags = [("turn", 2)] * 2 + [("sway", 2)] * 2 + [("drift", 2)] * 2
         outs = [psum.tile([P, half], F32, name="out_bank%d" % k, tag=tag, bufs=bufs) for k, (tag, bufs) in enumerate(tags)]
 
         def passes_b(h, b, codes, scales, start):

@@ -1,7 +1,6 @@
 from contextlib import ExitStack
 
 import concourse.mybir as mybir
-from concourse.masks import make_identity
 
 K, H, T, S, PICK, N = 512, 1024, 4096, 1024, 512, 384
 FLOPS = 2 * (3 * K * H * S + 2 * H * N * PICK)
@@ -22,6 +21,7 @@ PACK = 4
 PASS = P * PACK
 BANK = 512
 BLOCKS = H // PASS
+BANKS = {"turn": 2, "sway": 2, "drift": 4}
 
 
 def tile_list_wandering_alert_features_kernel(
@@ -55,13 +55,13 @@ def tile_list_wandering_alert_features_kernel(
         nc.vector.memset(w4_s[:].bitcast(I32), 0)
 
         def load_w(w, b, name):
-            raw = keep.tile([P, PACK, PASS], F32, name=name)
-            nc.sync.dma_start(out=raw[:], in_=w[:, b * PASS : (b + 1) * PASS].rearrange("(p j) c -> p j c", j=PACK))
+            raw = keep.tile([P, PACK * PASS], F32, name=name, align_bytes=64)
+            nc.sync.dma_start(out=raw[:].rearrange("p (j c) -> p j c", j=PACK), in_=w[:, b * PASS : (b + 1) * PASS].rearrange("(p j) c -> p j c", j=PACK))
             return raw
 
         def load_rows(x, b, name):
-            raw = keep.tile([P, PACK, x.shape[1]], F32, name=name)
-            nc.sync.dma_start(out=raw[:], in_=x[b * PASS : (b + 1) * PASS, :].rearrange("(p j) c -> p j c", j=PACK))
+            raw = keep.tile([P, PACK * x.shape[1]], F32, name=name, align_bytes=64)
+            nc.sync.dma_start(out=raw[:], in_=x[b * PASS : (b + 1) * PASS, :].rearrange("(p j) c -> p (j c)", j=PACK))
             return raw
 
         nc.sync.dma_start(offs_sb[:], offs)
@@ -93,24 +93,27 @@ def tile_list_wandering_alert_features_kernel(
             width = grouped.shape[1] // PACK
             codes = keep.tile([P, width], U32, name=name + "_c", align_bytes=64)
             scales = keep.tile([P, width], U8, name=name + "_s", align_bytes=64)
-            nc.vector.quantize_mx(out=codes[:].bitcast(FP8X4), scales=scales[:], in_=grouped[:])
+            nc.vector.quantize_mx(out=codes[:].bitcast(FP8X4), scales=scales[:], in_=grouped)
             return codes, scales
 
-        def deal_weight(engine, raw):
-            grouped = ring.tile([P, PACK * PASS], BF16, name="w_grouped", align_bytes=64)
+        def fresh(name, width, bufs):
+            return ring.tile([P, width], BF16, name=name, align_bytes=64, bufs=bufs)[:]
+
+        def plane(raw, first, count):
+            return raw[:, first * PICK : (first + count) * PICK]
+
+        def deal_weight(engine, raw, grouped):
             copy_on(
                 engine,
-                grouped[:].rearrange("p (t m j) -> p m t j", t=PACK, j=PACK),
-                raw[:].rearrange("p j (m t) -> p m t j", t=PACK),
+                grouped.rearrange("p (t m j) -> p m j t", t=PACK, j=PACK),
+                raw[:].rearrange("p (j m t) -> p m j t", j=PACK, t=PACK),
             )
             return grouped
 
-        def interleave(engine, planes, name):
-            width = planes.shape[2]
-            grouped = ring.tile([P, PACK * width], BF16, name=name, align_bytes=64)
+        def interleave(engine, planes, grouped):
             copy_on(
                 engine,
-                grouped[:].rearrange("p (c i t) -> p c t i", i=4, t=PACK),
+                grouped.rearrange("p (c i t) -> p c t i", i=4, t=PACK),
                 planes.rearrange("p t (c i) -> p c t i", i=4),
             )
             return grouped
@@ -118,10 +121,10 @@ def tile_list_wandering_alert_features_kernel(
         w2_w = keep.tile([P, 2 * H], U8, name="w2_w", align_bytes=64)
         w2_s = keep.tile([P, H], U8, name="w2_s", align_bytes=64)
         nc.vector.tensor_copy(
-            out=w2_w[:].bitcast(U16).rearrange("p (b t m) -> p b m t", b=BLOCKS, t=PACK),
-            in_=w2_raw[:].bitcast(U16).rearrange("p (b m t) -> p b m t", b=BLOCKS, t=PACK),
+            out=w2_w[:].bitcast(U16).rearrange("p (b t m) -> p b t m", b=BLOCKS, t=PACK),
+            in_=w2_raw[:].bitcast(U16).rearrange("p (b m t) -> p b t m", b=BLOCKS, t=PACK),
         )
-        w1_grouped = deal_weight(nc.scalar, w1_raw[0])
+        w1_grouped = deal_weight(nc.scalar, w1_raw[0], fresh("w_grouped", PACK * PASS, 2))
 
         v_s = [keep.tile([P, BANK], U8, name="v_s%d" % h, align_bytes=64) for h in range(2)]
         v_w = [keep.tile([P, BANK], U32, name="v_w%d" % h, align_bytes=64) for h in range(2)]
@@ -133,68 +136,69 @@ def tile_list_wandering_alert_features_kernel(
         def deal_w2_scales(b):
             cs = slice(b * PASS, (b + 1) * PASS)
             nc.vector.tensor_copy(
-                out=w2_s[:, cs].rearrange("p (t m) -> p m t", t=PACK),
-                in_=w2_sraw[:, cs].rearrange("p (m t) -> p m t", t=PACK),
+                out=w2_s[:, cs].rearrange("p (t m) -> p t m", t=PACK),
+                in_=w2_sraw[:, cs].rearrange("p (m t) -> p t m", t=PACK),
             )
 
         nc.vector.tensor_copy(v_w[0][:], tab_w[:].indirect(offs_sb[:, 0:cols]))
         deal_w2_scales(0)
         nc.vector.tensor_copy(v_w[1][:], tab_w[:].indirect(offs_sb[:, cols : 2 * cols]))
-        w3_q = [quantise(deal_weight(nc.vector, w3_raw[0]), "w3q0")]
+        w3_q = [quantise(deal_weight(nc.vector, w3_raw[0], fresh("w_grouped", PACK * PASS, 2)), "w3q0")]
 
-        ident = keep.tile([P, P], F32, name="ident")
-        make_identity(nc, ident[:])
-
-        def first_stage(i, h, top):
+        def weights(i):
             b, t = divmod(i, PACK)
             m = slice(t * P, (t + 1) * P)
-            hs = slice(h * BANK, (h + 1) * BANK)
-            turn = psum.tile([P, BANK], F32, name="turn", tag="turn", bufs=2)
-            sway = psum.tile([P, BANK], F32, name="sway", tag="sway", bufs=2)
-            drift = psum.tile([P, BANK], F32, name="drift", tag="drift", bufs=2)
-            for bank, words, scales in (
-                (turn, w1_q[b][0][:, m].bitcast(FP8X4), w1_q[b][1][:, m]),
-                (sway, w2_w[:, 2 * i * P : 2 * (i + 1) * P].bitcast(FP4X4), w2_s[:, i * P : (i + 1) * P]),
-            ):
-                for q in range(BANK // P):
-                    js = slice(q * P, (q + 1) * P)
-                    nc.tensor.matmul_mx(
-                        out=bank[:, js], lhsT=v_w[h][:, js].bitcast(FP8X4), lhsT_scale=v_s[h][:, js],
-                        rhs=words, rhs_scale=scales, start=True, stop=True,
-                    )
+            return (
+                (w1_q[b][0][:, m].bitcast(FP8X4), w1_q[b][1][:, m]),
+                (w2_w[:, 2 * i * P : 2 * (i + 1) * P].bitcast(FP4X4), w2_s[:, i * P : (i + 1) * P]),
+                (w3_q[b][0][:, m].bitcast(FP8X4), w3_q[b][1][:, m]),
+            )
+
+        def product(tag, weight, h):
+            bank = psum.tile([P, BANK], F32, name=tag, tag=tag, bufs=BANKS[tag])
             nc.tensor.matmul_mx(
-                out=drift[:], lhsT=w3_q[b][0][:, m].bitcast(FP8X4), lhsT_scale=w3_q[b][1][:, m],
+                out=bank[:], lhsT=weight[0], lhsT_scale=weight[1],
                 rhs=v_w[h][:].bitcast(FP8X4), rhs_scale=v_s[h][:], start=True, stop=True,
             )
-            th = ring.tile([P, BANK], F32, name="th", bufs=3)
-            ab = ring.tile([P, BANK], F32, name="ab", bufs=3)
-            nc.scalar.activation(out=th[:], in_=turn[:], func=ACT.Tanh)
-            nc.scalar.activation(out=ab[:], in_=sway[:], func=ACT.Abs)
-            nc.scalar.copy(out=top[:, hs], in_=drift[:])
+            return bank
+
+        def unary(i):
+            w_turn, w_sway, w_drift = weights(i)
+            th = ring.tile([P, S], F32, name="th", bufs=2)
+            ab = ring.tile([P, S], F32, name="ab", bufs=2)
+            for h in range(2):
+                hs = slice(h * BANK, (h + 1) * BANK)
+                nc.scalar.activation(out=th[:, hs], in_=product("turn", w_turn, h)[:], func=ACT.Tanh)
+                nc.scalar.activation(out=ab[:, hs], in_=product("sway", w_sway, h)[:], func=ACT.Abs)
             return th, ab
 
-        def maximum(h, top, th, ab):
-            hs = slice(h * BANK, (h + 1) * BANK)
-            total = psum.tile([P, BANK], F32, name="total", bufs=2)
-            for q in range(BANK // P):
-                js = slice(q * P, (q + 1) * P)
-                nc.tensor.matmul(total[:, js], lhsT=th[:, js], rhs=ident[:], is_transpose=True, start=True, stop=False)
-                nc.tensor.matmul(total[:, js], lhsT=ab[:, js], rhs=ident[:], is_transpose=True, start=False, stop=True)
-            nc.vector.tensor_tensor(out=top[:, hs], in0=total[:], in1=top[:, hs], op=ALU.max)
+        def add(th, ab):
+            top = ring.tile([P, S], F32, name="top", bufs=3)
+            nc.vector.tensor_tensor(out=top[:], in0=th[:], in1=ab[:], op=ALU.add)
+            return top
+
+        def maximum(i, top):
+            for h in range(2):
+                hs = slice(h * BANK, (h + 1) * BANK)
+                drift = product("drift", weights(i)[2], h)
+                nc.vector.tensor_tensor(out=top[:, hs], in0=drift[:], in1=top[:, hs], op=ALU.max)
 
         xa_planes = [keep.tile([P, PACK, PICK], BF16, name="xa_planes%d" % b) for b in range(BLOCKS)]
         xb_planes = [keep.tile([P, PACK, PICK], F32, name="xb_planes%d" % b) for b in range(BLOCKS)]
 
         def scale_garden(i):
             b, t = divmod(i, PACK)
-            gg = ring.tile([P, PICK], F32, name="gg", bufs=4)
-            nc.scalar.activation(out=gg[:], in_=garden_sb[b][:, t, :], func=ACT.Copy, scale=gain_sb[:, b, t : t + 1])
+            gg = plane(w3_raw[0], t, 1)
+            nc.scalar.activation(out=gg, in_=plane(garden_sb[b], t, 1), func=ACT.Copy, scale=gain_sb[:, b, t : t + 1])
             return gg
 
-        def pick_a(i, top, c0, c1):
-            b, t = divmod(i, PACK)
-            ga = ring.tile([P, c1 - c0], F32, name="ga")
+        def pick_a(top, c0, c1):
+            ga = ring.tile([P, c1 - c0], F32, name="ga", tag="ga%d" % (c1 - c0), bufs=1 if c1 - c0 == PICK else 2)
             nc.vector.tensor_copy(ga[:], top[:].indirect(pos1_sb[:, c0 // 16 : c1 // 16]))
+            return ga
+
+        def shift_a(i, ga, c0, c1):
+            b, t = divmod(i, PACK)
             nc.scalar.activation(
                 out=xa_planes[b][:, t, c0:c1], in_=ga[:], func=ACT.Identity,
                 scale=gain_sb[:, b, t : t + 1], bias=corr_sb[:, b, t : t + 1],
@@ -206,43 +210,39 @@ def tile_list_wandering_alert_features_kernel(
                 xb_planes[b][:, t, c0:c1], top[:].indirect(pos2_sb[:, c0 // 16 : c1 // 16]), gg[:, c0:c1], ALU.mult
             )
 
-        w5_q = []
         tiles = BLOCKS * PACK
-        tops = {}
-        ggs = {}
-        parts = {}
-        for k in range(2 * tiles + 1):
-            i, h = divmod(k, 2)
-            if i < tiles:
-                if h == 0:
-                    tops[i] = ring.tile([P, S], F32, name="top", bufs=3)
-                parts[k] = first_stage(i, h, tops[i])
-            if k >= 1:
-                maximum((k - 1) % 2, tops[(k - 1) // 2], *parts[k - 1])
-            if h == 0 and i < tiles:
-                ggs[i] = scale_garden(i)
-            if h == 1 and i >= 1:
-                pick_a(i - 1, tops[i - 1], 0, PICK)
-            if k == 1:
-                deal_w2_scales(1)
-            if k == 3:
-                w1_q.append(quantise(deal_weight(nc.vector, w1_raw[1]), "w1q1"))
-            if k == 5:
-                w3_q.append(quantise(deal_weight(nc.vector, w3_raw[1]), "w3q1"))
-            if k == 11:
-                xa0 = quantise(interleave(nc.vector, xa_planes[0][:], "xa_grouped"), "xaq0")
-            if k == 13:
-                xb0 = quantise(interleave(nc.vector, xb_planes[0][:], "xb_grouped"), "xbq0")
-            if k == 7:
-                w5_q.append(quantise(interleave(nc.scalar, w5_raw[0][:], "w5_grouped0"), "w5q0"))
-            if k == 9:
-                w5_q.append(quantise(interleave(nc.scalar, w5_raw[1][:], "w5_grouped1"), "w5q1"))
-            if h == 0 and 2 <= i:
-                pick_b(i - 2, tops[i - 2], ggs[i - 2], 0, PICK)
+        tops = {0: add(*unary(0))}
+        deal_w2_scales(1)
+        maximum(0, tops[0])
+        w5_q = []
+        stage = plane(garden_sb[0], 0, 2).bitcast(BF16)
+        for i in range(tiles - 1):
+            parts = unary(i + 1)
+            if i >= 1:
+                shift_a(i - 1, ga, 0, PICK)
+            gg = scale_garden(i)
+            tops[i + 1] = add(*parts)
+            ga = pick_a(tops[i], 0, PICK)
+            maximum(i + 1, tops[i + 1])
+            pick_b(i, tops[i], gg, 0, PICK)
+            if i == 1:
+                w1_q.append(quantise(deal_weight(nc.scalar, w1_raw[1], stage), "w1q1"))
+            if i == 2:
+                w3_q.append(quantise(deal_weight(nc.scalar, w3_raw[1], stage), "w3q1"))
+            if i in (3,4):
+                b = len(w5_q)
+                rows = w5_raw[b][:].rearrange("p (j n) -> p j n", j=PACK)
+                w5_q.append(quantise(interleave(nc.scalar, rows, stage[:, : PACK * N]), "w5q%d" % b))
+            if i == 5:
+                xb0 = quantise(interleave(nc.scalar, xb_planes[0][:], fresh("xb_grouped", PACK * PICK, 1)), "xbq0")
+            if i == 6:
+                xa0 = quantise(interleave(nc.scalar, xa_planes[0][:], fresh("xa_grouped", PACK * PICK, 1)), "xaq0")
+        shift_a(tiles - 2, ga, 0, PICK)
+        gg = scale_garden(tiles - 1)
 
         half = PICK // 2
         last = tiles - 1
-        tags = [("turn", 2)] * 2 + [("sway", 2)] * 2 + [("drift", 2)] * 2
+        tags = [(tag, BANKS[tag]) for tag in BANKS for k in range(BANKS[tag])][:6]
         outs = [psum.tile([P, half], F32, name="out_bank%d" % k, tag=tag, bufs=bufs) for k, (tag, bufs) in enumerate(tags)]
 
         def passes_b(h, b, codes, scales, start):
@@ -265,23 +265,29 @@ def tile_list_wandering_alert_features_kernel(
             hs = slice(h * half, (h + 1) * half)
             passes_b(h, 0, xb0[0][:, hs], xb0[1][:, hs], True)
             passes_a(h, 0, xa0[0][:, hs], xa0[1][:, hs], False)
-        for h in range(2):
-            pick_a(last, tops[last], h * half, (h + 1) * half)
-            pick_b(last, tops[last], ggs[last], h * half, (h + 1) * half)
-        grouped = []
-        for h in range(2):
-            hs = slice(h * half, (h + 1) * half)
-            grouped.append((
-                interleave(nc.scalar, xa_planes[1][:, :, hs], "xa_grouped"),
-                interleave(nc.vector, xb_planes[1][:, :, hs], "xb_grouped"),
-            ))
-        for h in range(2):
-            hs = slice(h * half, (h + 1) * half)
-            xb1 = quantise(grouped[h][1], "xbq1%d" % h)
-            xa1 = quantise(grouped[h][0], "xaq1%d" % h)
+        halves = [slice(h * half, (h + 1) * half) for h in range(2)]
+
+        def group_a(h):
+            shift_a(last, pick_a(tops[last], h * half, (h + 1) * half), h * half, (h + 1) * half)
+            return interleave(nc.scalar, xa_planes[1][:, :, halves[h]], fresh("xa_last", PACK * half, 2))
+
+        def group_b(h):
+            return interleave(nc.vector, xb_planes[1][:, :, halves[h]], fresh("xb_last", PACK * half, 2))
+
+        def finish(h, xa_grouped, xb_grouped):
+            xb1 = quantise(xb_grouped, "xbq1%d" % h)
+            xa1 = quantise(xa_grouped, "xaq1%d" % h)
             passes_b(h, 1, xb1[0][:], xb1[1][:], False)
             passes_a(h, 1, xa1[0][:], xa1[1][:], True)
             for n in range(N // P):
                 res = ring.tile([P, half], F32, name="res", bufs=6)
                 copy_on(nc.vector if (h == 1 and n == 1) else nc.scalar, res[:], outs[3 * h + n][:])
-                nc.sync.dma_start(out=out[n * P : (n + 1) * P, hs], in_=res[:])
+                nc.sync.dma_start(out=out[n * P : (n + 1) * P, halves[h]], in_=res[:])
+
+        xa_low = group_a(0)
+        pick_b(last, tops[last], gg, 0, half)
+        xa_high = group_a(1)
+        xb_low = group_b(0)
+        pick_b(last, tops[last], gg, half, PICK)
+        finish(0, xa_low, xb_low)
+        finish(1, xa_high, group_b(1))

@@ -192,16 +192,24 @@ def tile_list_wandering_alert_features_kernel(
             nc.scalar.activation(out=gg, in_=plane(garden_sb[b], t, 1), func=ACT.Copy, scale=gain_sb[:, b, t : t + 1])
             return gg
 
-        def pick_a(top, c0, c1):
-            ga = ring.tile([P, c1 - c0], F32, name="ga", tag="ga%d" % (c1 - c0), bufs=1 if c1 - c0 == PICK else 2)
-            nc.vector.tensor_copy(ga[:], top[:].indirect(pos1_sb[:, c0 // 16 : c1 // 16]))
+        def pick_a(i, top, c0, c1):
+            b, t = divmod(i, PACK)
+            ga = plane(garden_sb[b], t, 1)[:, c0:c1]
+            nc.vector.tensor_copy(ga, top[:].indirect(pos1_sb[:, c0 // 16 : c1 // 16]))
             return ga
 
         def shift_a(i, ga, c0, c1):
             b, t = divmod(i, PACK)
             nc.scalar.activation(
-                out=xa_planes[b][:, t, c0:c1], in_=ga[:], func=ACT.Identity,
+                out=xa_planes[b][:, t, c0:c1], in_=ga, func=ACT.Identity,
                 scale=gain_sb[:, b, t : t + 1], bias=corr_sb[:, b, t : t + 1],
+            )
+
+        def shift_a_pool(i, ga):
+            b, t = divmod(i, PACK)
+            nc.gpsimd.tensor_scalar(
+                out=xa_planes[b][:, t, :], in0=ga, scalar1=gain_sb[:, b, t : t + 1],
+                scalar2=corr_sb[:, b, t : t + 1], op0=ALU.mult, op1=ALU.add,
             )
 
         def pick_b(i, top, gg, c0, c1):
@@ -218,15 +226,13 @@ def tile_list_wandering_alert_features_kernel(
         stage = plane(garden_sb[0], 0, 2).bitcast(BF16)
         for i in range(tiles - 1):
             parts = unary(i + 1)
-            if i >= 1:
-                shift_a(i - 1, ga, 0, PICK)
             gg = scale_garden(i)
             tops[i + 1] = add(*parts)
-            ga = pick_a(tops[i], 0, PICK)
+            shift_a_pool(i, pick_a(i, tops[i], 0, PICK))
             maximum(i + 1, tops[i + 1])
             pick_b(i, tops[i], gg, 0, PICK)
-            if i == 1:
-                w1_q.append(quantise(deal_weight(nc.scalar, w1_raw[1], stage), "w1q1"))
+            if i == 0:
+                w1_q.append(quantise(deal_weight(nc.scalar, w1_raw[1], plane(w3_raw[0], 2, 2).bitcast(BF16)), "w1q1"))
             if i == 2:
                 w3_q.append(quantise(deal_weight(nc.scalar, w3_raw[1], stage), "w3q1"))
             if i in (3,4):
@@ -237,7 +243,6 @@ def tile_list_wandering_alert_features_kernel(
                 xb0 = quantise(interleave(nc.scalar, xb_planes[0][:], fresh("xb_grouped", PACK * PICK, 1)), "xbq0")
             if i == 6:
                 xa0 = quantise(interleave(nc.scalar, xa_planes[0][:], fresh("xa_grouped", PACK * PICK, 1)), "xaq0")
-        shift_a(tiles - 2, ga, 0, PICK)
         gg = scale_garden(tiles - 1)
 
         half = PICK // 2
@@ -268,7 +273,7 @@ def tile_list_wandering_alert_features_kernel(
         halves = [slice(h * half, (h + 1) * half) for h in range(2)]
 
         def group_a(h):
-            shift_a(last, pick_a(tops[last], h * half, (h + 1) * half), h * half, (h + 1) * half)
+            shift_a(last, pick_a(last, tops[last], h * half, (h + 1) * half), h * half, (h + 1) * half)
             return interleave(nc.scalar, xa_planes[1][:, :, halves[h]], fresh("xa_last", PACK * half, 2))
 
         def group_b(h):

from contextlib import ExitStack

import concourse.mybir as mybir

K, H, T, S, PICK, N = 512, 1024, 4096, 1024, 512, 384
FLOPS = 2 * (3 * K * H * S + 2 * H * N * PICK)

F32 = mybir.dt.float32
BF16 = mybir.dt.bfloat16
I32 = mybir.dt.int32
U32 = mybir.dt.uint32
U16 = mybir.dt.uint16
U8 = mybir.dt.uint8
FP8X4 = mybir.dt.float8_e4m3fn_x4
FP4X4 = mybir.dt.float4_e2m1fn_x4
ACT = mybir.ActivationFunctionType
ALU = mybir.AluOpType

P = 128
PACK = 4
PASS = P * PACK
BANK = 512
BLOCKS = H // PASS
BANKS = {"turn": 2, "sway": 2, "drift": 4}


def tile_list_wandering_alert_features_kernel(
    tc, tab_words, tab_scales, offs, pos1, pos2, w1, w2_words, w2_scales, w3,
    gain, corridor, garden, w4_words, w4_scales, w5, out,
):
    nc = tc.nc
    with ExitStack() as ctx:
        keep = ctx.enter_context(tc.tile_pool(name="keep", bufs=1))
        ring = ctx.enter_context(tc.tile_pool(name="ring", bufs=2))
        psum = ctx.enter_context(tc.psum_pool(name="psum", bufs=1))

        def load_scale_rows(queue, plane, rows):
            for q in range(4):
                queue.dma_start(out=plane[32 * q : 32 * q + 4].bitcast(I32), in_=rows[4 * q : 4 * q + 4].bitcast(I32))

        offs_sb = keep.tile([P, S // 16], U16, name="offs_sb")
        pos1_sb = keep.tile([P, PICK // 16], U16, name="pos1_sb")
        pos2_sb = keep.tile([P, PICK // 16], U16, name="pos2_sb")
        tab_w = keep.tile([P, T], U32, name="tab_w", align_bytes=64)
        tab_s = keep.tile([P, T], U8, name="tab_s", align_bytes=64)
        w2_raw = keep.tile([P, 2 * H], U8, name="w2_raw", align_bytes=64)
        w2_sraw = keep.tile([P, H], U8, name="w2_sraw", align_bytes=64)
        w4_w = keep.tile([P, BLOCKS, 2 * N], U8, name="w4_w", align_bytes=64)
        w4_s = keep.tile([P, BLOCKS, N], U8, name="w4_s", align_bytes=64)
        gain_sb = keep.tile([P, BLOCKS, PACK], F32, name="gain_sb")
        corr_sb = keep.tile([P, BLOCKS, PACK], F32, name="corr_sb")

        nc.vector.memset(tab_s[:].bitcast(I32), 0)
        nc.vector.memset(w2_sraw[:].bitcast(I32), 0)
        nc.vector.memset(w4_s[:].bitcast(I32), 0)

        def load_w(w, b, name):
            raw = keep.tile([P, PACK * PASS], F32, name=name, align_bytes=64)
            nc.sync.dma_start(out=raw[:].rearrange("p (j c) -> p j c", j=PACK), in_=w[:, b * PASS : (b + 1) * PASS].rearrange("(p j) c -> p j c", j=PACK))
            return raw

        def load_rows(x, b, name):
            raw = keep.tile([P, PACK * x.shape[1]], F32, name=name, align_bytes=64)
            nc.sync.dma_start(out=raw[:], in_=x[b * PASS : (b + 1) * PASS, :].rearrange("(p j) c -> p (j c)", j=PACK))
            return raw

        nc.sync.dma_start(offs_sb[:], offs)
        nc.sync.dma_start(out=w2_raw[:].bitcast(I32), in_=w2_words[0].bitcast(I32))
        w1_raw = [load_w(w1, 0, "w1_raw0")]
        load_scale_rows(nc.sync, tab_s, tab_scales[0])
        nc.sync.dma_start(out=tab_w[:].bitcast(I32), in_=tab_words[0].rearrange("p n t -> p (n t)").bitcast(I32))
        load_scale_rows(nc.sync, w2_sraw, w2_scales[0])
        w3_raw = [load_w(w3, 0, "w3_raw0")]
        nc.sync.dma_start(pos1_sb[:], pos1)
        nc.sync.dma_start(pos2_sb[:], pos2)
        nc.sync.dma_start(out=gain_sb[:], in_=gain.rearrange("(b p t) -> p b t", b=BLOCKS, t=PACK))
        nc.sync.dma_start(out=corr_sb[:], in_=corridor.rearrange("(b p t) -> p b t", b=BLOCKS, t=PACK))
        garden_sb = [load_rows(garden, 0, "garden0")]
        w1_raw.append(load_w(w1, 1, "w1_raw1"))
        w3_raw.append(load_w(w3, 1, "w3_raw1"))
        garden_sb.append(load_rows(garden, 1, "garden1"))
        w5_raw = [load_rows(w5, b, "w5_raw%d" % b) for b in range(BLOCKS)]
        nc.sync.dma_start(out=w4_w[:].bitcast(I32), in_=w4_words.rearrange("a p n -> p a n").bitcast(I32))
        load_scale_rows(nc.sync, w4_s, w4_scales.rearrange("a r n -> r a n"))

        def copy_on(engine, dst, src):
            if engine is nc.scalar:
                nc.scalar.copy(out=dst, in_=src)
            else:
                engine.tensor_copy(out=dst, in_=src)

        def quantise(grouped, name):
            width = grouped.shape[1] // PACK
            codes = keep.tile([P, width], U32, name=name + "_c", align_bytes=64)
            scales = keep.tile([P, width], U8, name=name + "_s", align_bytes=64)
            nc.vector.quantize_mx(out=codes[:].bitcast(FP8X4), scales=scales[:], in_=grouped)
            return codes, scales

        def fresh(name, width, bufs):
            return ring.tile([P, width], BF16, name=name, align_bytes=64, bufs=bufs)[:]

        def plane(raw, first, count):
            return raw[:, first * PICK : (first + count) * PICK]

        def deal_weight(engine, raw, grouped):
            copy_on(
                engine,
                grouped.rearrange("p (t m j) -> p m j t", t=PACK, j=PACK),
                raw[:].rearrange("p (j m t) -> p m j t", j=PACK, t=PACK),
            )
            return grouped

        def interleave(engine, planes, grouped):
            copy_on(
                engine,
                grouped.rearrange("p (c i t) -> p c t i", i=4, t=PACK),
                planes.rearrange("p t (c i) -> p c t i", i=4),
            )
            return grouped

        w2_w = keep.tile([P, 2 * H], U8, name="w2_w", align_bytes=64)
        w2_s = keep.tile([P, H], U8, name="w2_s", align_bytes=64)
        nc.vector.tensor_copy(
            out=w2_w[:].bitcast(U16).rearrange("p (b t m) -> p b t m", b=BLOCKS, t=PACK),
            in_=w2_raw[:].bitcast(U16).rearrange("p (b m t) -> p b t m", b=BLOCKS, t=PACK),
        )
        w1_grouped = deal_weight(nc.scalar, w1_raw[0], fresh("w_grouped", PACK * PASS, 2))

        v_s = [keep.tile([P, BANK], U8, name="v_s%d" % h, align_bytes=64) for h in range(2)]
        v_w = [keep.tile([P, BANK], U32, name="v_w%d" % h, align_bytes=64) for h in range(2)]
        cols = BANK // 16
        for h in range(2):
            nc.vector.tensor_copy(v_s[h][:], tab_s[:].indirect(offs_sb[:, h * cols : (h + 1) * cols]))
        w1_q = [quantise(w1_grouped, "w1q0")]

        def deal_w2_scales(b):
            cs = slice(b * PASS, (b + 1) * PASS)
            nc.vector.tensor_copy(
                out=w2_s[:, cs].rearrange("p (t m) -> p t m", t=PACK),
                in_=w2_sraw[:, cs].rearrange("p (m t) -> p t m", t=PACK),
            )

        nc.vector.tensor_copy(v_w[0][:], tab_w[:].indirect(offs_sb[:, 0:cols]))
        deal_w2_scales(0)
        nc.vector.tensor_copy(v_w[1][:], tab_w[:].indirect(offs_sb[:, cols : 2 * cols]))
        w3_q = [quantise(deal_weight(nc.vector, w3_raw[0], fresh("w_grouped", PACK * PASS, 2)), "w3q0")]

        def weights(i):
            b, t = divmod(i, PACK)
            m = slice(t * P, (t + 1) * P)
            return (
                (w1_q[b][0][:, m].bitcast(FP8X4), w1_q[b][1][:, m]),
                (w2_w[:, 2 * i * P : 2 * (i + 1) * P].bitcast(FP4X4), w2_s[:, i * P : (i + 1) * P]),
                (w3_q[b][0][:, m].bitcast(FP8X4), w3_q[b][1][:, m]),
            )

        def product(tag, weight, h):
            bank = psum.tile([P, BANK], F32, name=tag, tag=tag, bufs=BANKS[tag])
            nc.tensor.matmul_mx(
                out=bank[:], lhsT=weight[0], lhsT_scale=weight[1],
                rhs=v_w[h][:].bitcast(FP8X4), rhs_scale=v_s[h][:], start=True, stop=True,
            )
            return bank

        def unary(i):
            w_turn, w_sway, w_drift = weights(i)
            th = ring.tile([P, S], F32, name="th", bufs=2)
            ab = ring.tile([P, S], F32, name="ab", bufs=2)
            for h in range(2):
                hs = slice(h * BANK, (h + 1) * BANK)
                nc.scalar.activation(out=th[:, hs], in_=product("turn", w_turn, h)[:], func=ACT.Tanh)
                nc.scalar.activation(out=ab[:, hs], in_=product("sway", w_sway, h)[:], func=ACT.Abs)
            return th, ab

        def add(th, ab):
            top = ring.tile([P, S], F32, name="top", bufs=3)
            nc.vector.tensor_tensor(out=top[:], in0=th[:], in1=ab[:], op=ALU.add)
            return top

        def maximum(i, top):
            for h in range(2):
                hs = slice(h * BANK, (h + 1) * BANK)
                drift = product("drift", weights(i)[2], h)
                nc.vector.tensor_tensor(out=top[:, hs], in0=drift[:], in1=top[:, hs], op=ALU.max)

        xa_planes = [keep.tile([P, PACK, PICK], BF16, name="xa_planes%d" % b) for b in range(BLOCKS)]
        xb_planes = [keep.tile([P, PACK, PICK], F32, name="xb_planes%d" % b) for b in range(BLOCKS)]

        def scale_garden(i):
            b, t = divmod(i, PACK)
            gg = plane(w3_raw[0], t, 1)
            nc.scalar.activation(out=gg, in_=plane(garden_sb[b], t, 1), func=ACT.Copy, scale=gain_sb[:, b, t : t + 1])
            return gg

        def pick_a(i, top, c0, c1):
            b, t = divmod(i, PACK)
            ga = plane(garden_sb[b], t, 1)[:, c0:c1]
            nc.vector.tensor_copy(ga, top[:].indirect(pos1_sb[:, c0 // 16 : c1 // 16]))
            return ga

        def shift_a(i, ga, c0, c1):
            b, t = divmod(i, PACK)
            nc.scalar.activation(
                out=xa_planes[b][:, t, c0:c1], in_=ga, func=ACT.Identity,
                scale=gain_sb[:, b, t : t + 1], bias=corr_sb[:, b, t : t + 1],
            )

        def shift_a_pool(i, ga):
            b, t = divmod(i, PACK)
            nc.gpsimd.tensor_scalar(
                out=xa_planes[b][:, t, :], in0=ga, scalar1=gain_sb[:, b, t : t + 1],
                scalar2=corr_sb[:, b, t : t + 1], op0=ALU.mult, op1=ALU.add,
            )

        def pick_b(i, top, gg, c0, c1):
            b, t = divmod(i, PACK)
            nc.vector.tensor_tensor(
                xb_planes[b][:, t, c0:c1], top[:].indirect(pos2_sb[:, c0 // 16 : c1 // 16]), gg[:, c0:c1], ALU.mult
            )

        tiles = BLOCKS * PACK
        tops = {0: add(*unary(0))}
        deal_w2_scales(1)
        maximum(0, tops[0])
        w5_q = []
        stage = plane(garden_sb[0], 0, 2).bitcast(BF16)
        for i in range(tiles - 1):
            parts = unary(i + 1)
            gg = scale_garden(i)
            tops[i + 1] = add(*parts)
            shift_a_pool(i, pick_a(i, tops[i], 0, PICK))
            maximum(i + 1, tops[i + 1])
            pick_b(i, tops[i], gg, 0, PICK)
            if i == 0:
                w1_q.append(quantise(deal_weight(nc.scalar, w1_raw[1], plane(w3_raw[0], 2, 2).bitcast(BF16)), "w1q1"))
            if i == 2:
                w3_q.append(quantise(deal_weight(nc.scalar, w3_raw[1], stage), "w3q1"))
            if i in (3,4):
                b = len(w5_q)
                rows = w5_raw[b][:].rearrange("p (j n) -> p j n", j=PACK)
                w5_q.append(quantise(interleave(nc.scalar, rows, stage[:, : PACK * N]), "w5q%d" % b))
            if i == 5:
                xb0 = quantise(interleave(nc.scalar, xb_planes[0][:], fresh("xb_grouped", PACK * PICK, 1)), "xbq0")
            if i == 6:
                xa0 = quantise(interleave(nc.scalar, xa_planes[0][:], fresh("xa_grouped", PACK * PICK, 1)), "xaq0")
        gg = scale_garden(tiles - 1)

        half = PICK // 2
        last = tiles - 1
        tags = [(tag, BANKS[tag]) for tag in BANKS for k in range(BANKS[tag])][:6]
        outs = [psum.tile([P, half], F32, name="out_bank%d" % k, tag=tag, bufs=bufs) for k, (tag, bufs) in enumerate(tags)]

        def passes_b(h, b, codes, scales, start):
            for n in range(N // P):
                m = slice(n * P, (n + 1) * P)
                nc.tensor.matmul_mx(
                    out=outs[3 * h + n][:], lhsT=w5_q[b][0][:, m].bitcast(FP8X4), lhsT_scale=w5_q[b][1][:, m],
                    rhs=codes.bitcast(FP8X4), rhs_scale=scales, start=start, stop=False,
                )

        def passes_a(h, b, codes, scales, stop):
            for n in range(N // P):
                nc.tensor.matmul_mx(
                    out=outs[3 * h + n][:], lhsT=w4_w[:, b, 2 * n * P : 2 * (n + 1) * P].bitcast(FP4X4),
                    lhsT_scale=w4_s[:, b, n * P : (n + 1) * P],
                    rhs=codes.bitcast(FP8X4), rhs_scale=scales, start=False, stop=stop,
                )

        for h in range(2):
            hs = slice(h * half, (h + 1) * half)
            passes_b(h, 0, xb0[0][:, hs], xb0[1][:, hs], True)
            passes_a(h, 0, xa0[0][:, hs], xa0[1][:, hs], False)
        halves = [slice(h * half, (h + 1) * half) for h in range(2)]

        def group_a(h):
            shift_a(last, pick_a(last, tops[last], h * half, (h + 1) * half), h * half, (h + 1) * half)
            return interleave(nc.scalar, xa_planes[1][:, :, halves[h]], fresh("xa_last", PACK * half, 2))

        def group_b(h):
            return interleave(nc.vector, xb_planes[1][:, :, halves[h]], fresh("xb_last", PACK * half, 2))

        def finish(h, xa_grouped, xb_grouped):
            xb1 = quantise(xb_grouped, "xbq1%d" % h)
            xa1 = quantise(xa_grouped, "xaq1%d" % h)
            passes_b(h, 1, xb1[0][:], xb1[1][:], False)
            passes_a(h, 1, xa1[0][:], xa1[1][:], True)
            for n in range(N // P):
                res = ring.tile([P, half], F32, name="res", bufs=6)
                copy_on(nc.vector if (h == 1 and n == 1) else nc.scalar, res[:], outs[3 * h + n][:])
                nc.sync.dma_start(out=out[n * P : (n + 1) * P, halves[h]], in_=res[:])

        xa_low = group_a(0)
        pick_b(last, tops[last], gg, 0, half)
        xa_high = group_a(1)
        xb_low = group_b(0)
        pick_b(last, tops[last], gg, half, PICK)
        finish(0, xa_low, xb_low)
        finish(1, xa_high, group_b(1))
